import numpy as np
CORES = [32,33,34,35,36,37,38,39,40,41,42,43,48,49]
N = 14
TK = 256
D = 128 * N
def setup_inputs(rng):
    return {"x": (rng.standard_normal((N, 128, TK), dtype=np.float32) + 2 * rng.standard_normal((N, 1, TK), dtype=np.float32))}
def reference(x):
    X = x.astype(np.float64)
    m = X.sum(axis=(0, 1)) / D
    s = ((X - m) ** 2).sum(axis=(0, 1)) / D
    return {"y": (X - m).astype(np.float32), "m": np.broadcast_to(m.astype(np.float32), (N, 1, TK)), "s": np.broadcast_to(s.astype(np.float32), (N, 1, TK))}

@@ -1,0 +1,195 @@
+from concourse.bass import DstId, RemoteDMATransfer
+from concourse.mybir import AluOpType
+
+NSIM = 64
+
+SCRATCH = {
+    "xs": ("sbuf", [128, 256], "float32"),
+    "sq": ("sbuf", [128, 256], "float32"),
+    "ys": ("sbuf", [128, 256], "float32"),
+    "invd": ("sbuf", [128, 4], "float32"),
+    "ones": ("sbuf", [128, 128], "float32"),
+    "st": ("sbuf", [128, 4], "float32"),
+    "G": ("sbuf", [128, 512], "float32"),
+    "tp": ("sbuf", [128, 8], "float32"),
+    "tot": ("sbuf", [128, 4], "float32"),
+    "msq": ("sbuf", [128, 4], "float32"),
+    "sv": ("sbuf", [128, 4], "float32"),
+    "coll": ("dram", [16, 128, 4], "float32"),
+    "gath": ("dram", [2, 128, 4], "float32"),
+    "pst": ("psum", [128, 512], "float32"),
+    "pta": ("psum", [128, 512], "float32"),
+    "pm0": ("psum", [128, 512], "float32"),
+    "pm1": ("psum", [128, 512], "float32"),
+}
+SEMAPHORES = ["cst", "ld", "sq0", "sq1", "mm1", "stc", "sent", "arr1", "own", "ge", "pa", "pac", "arr2", "gl", "tpl",
+              "tt", "tq", "ts", "m0", "m1", "y0", "y1", "outm", "outs", "outy0", "outy1"]
+
+
+def _bits(mask):
+    return [e for e in range(mask.bit_length()) if (mask >> e) & 1]
+
+
+def _hops(topo, a, b):
+    ca, cb = topo.chip(a), topo.chip(b)
+    if ca == cb:
+        return 0
+    return 1 if (topo.mates(ca, cb) or topo.same_plane(ca, cb)) else 2
+
+
+def _plan(T, topo):
+    ranks = list(T.cores)
+    by_chip = {}
+    for r in ranks:
+        by_chip.setdefault(topo.chip(r), []).append(r)
+    main = max(sorted(by_chip), key=lambda ch: len(by_chip[ch]))
+    groups = {}
+    for ch in sorted(by_chip):
+        home = main if (ch == main or topo.same_plane(ch, main)) else ch
+        groups.setdefault(home, []).extend(by_chip[ch])
+    relays = []
+    for home in sorted(groups):
+        mem = groups[home]
+        cand = [c for c in range(NSIM) if topo.chip(c) == home
+                and all(topo.may_write(c, r) for r in ranks if r != c)
+                and all(topo.may_write(m, c) for m in mem if m != c)]
+        cand.sort(key=lambda c: (c in ranks, -sum(1 for m in mem if topo.die(m) == topo.die(c)), c))
+        relays.append((cand[0], mem))
+    return relays
+
+
+def _fold_call(g, core, T, topo, slot, nsrc, dests):
+    load = {}
+    order = sorted(dests, key=lambda d: (-_hops(topo, core, d), d))
+    for d in order:
+        allowed = _bits(topo.mask(core, d))
+        onchip = _hops(topo, core, d) == 0
+        e = min(allowed, key=lambda k: (len(load.get(k, [])), -k if onchip else k))
+        load.setdefault(e, []).append(d)
+    transfers = []
+    for e in sorted(load):
+        ids = []
+        for d in load[e]:
+            rid, pid, _ = topo.addr(d)
+            ids.append(DstId(rid=rid, pnc=pid))
+        transfers.append(RemoteDMATransfer(dst_ids=ids, dma_engine_mask=1 << e, remote_sem=T.sem.arr2,
+                                           srcs=[T.coll[i] for i in range(nsrc)],
+                                           dsts=[T.gath[slot] for _ in load[e]], alu_op=1))
+    g.remote_dma_fused(transfers, local_sem=T.sem.sent)
+    return len(transfers)
+
+
+def rank_program(g, core, T, topo):
+    S = T.sem
+    ranks = list(T.cores)
+    relays = _plan(T, topo)
+    rank = T.rank_of(core)
+    my_slot = None
+    for k, (rc, mem) in enumerate(relays):
+        if rc == core:
+            my_slot = k
+    if rank is None and my_slot is None:
+        return
+    if my_slot is not None:
+        mem = relays[my_slot][1]
+        n1 = len(mem)
+        arr1_total = sum(len(_bits(topo.mask(m, core))) for m in mem if m != core)
+        dests = [r for r in ranks if r != core]
+
+    if rank is None:
+        g.wait_ge(S.arr1, arr1_total)
+        n = _fold_call(g, core, T, topo, my_slot, n1, dests)
+        g.wait_ge(S.sent, n)
+        return
+
+    sy, sc, te, ve = g.sync, g.scalar, g.tensor, g.vector
+    D = 128 * len(ranks)
+    for k, (rc, mem_k) in enumerate(relays):
+        if core in mem_k:
+            to_relay, my_idx = rc, mem_k.index(core)
+
+    sy.dma_start(T.xs[:], T.x[:]).then_inc(S.ld, 16)
+    ve.memset(T.invd[:], 1.0 / D).then_inc(S.cst, 1)
+    ve.memset(T.ones[:], 1.0).then_inc(S.cst, 1)
+
+    te.wait_ge(S.cst, 2)
+    te.wait_ge(S.ld, 16)
+    for jj in range(2):
+        te.matmul(T.pst[:, jj:jj + 1], T.xs[:, jj:256:2], T.invd[:, 0:1], True, True).then_inc(S.mm1, 1)
+    ve.wait_ge(S.ld, 16)
+    ve.tensor_tensor(T.sq[:, 0:128], T.xs[:, 0:256:2], T.xs[:, 0:256:2], AluOpType.mult).then_inc(S.sq0, 1)
+    ve.tensor_tensor(T.sq[:, 128:256], T.xs[:, 1:256:2], T.xs[:, 1:256:2], AluOpType.mult).then_inc(S.sq1, 1)
+    te.wait_ge(S.sq0, 1)
+    te.matmul(T.pst[:, 2:3], T.sq[:, 0:128], T.invd[:, 0:1], True, True).then_inc(S.mm1, 1)
+    te.wait_ge(S.sq1, 1)
+    te.matmul(T.pst[:, 3:4], T.sq[:, 128:256], T.invd[:, 0:1], True, True).then_inc(S.mm1, 1)
+    ve.wait_ge(S.mm1, 4)
+    ve.tensor_copy(T.st[:], T.pst[:, 0:4]).then_inc(S.stc, 1)
+
+    if my_slot is None:
+        g.wait_ge(S.stc, 1)
+        rid, pid, _ = topo.addr(to_relay)
+        mask = topo.mask(core, to_relay)
+        g.remote_dma(out_ap=T.coll[my_idx], in_ap=T.st[:], remote_sem=S.arr1, local_sem=S.sent, pid=pid,
+                     routing_id=rid, dma_engine_mask=mask)
+        sent = len(_bits(mask))
+        K = len(relays)
+        sy.wait_ge(S.arr2, K)
+        sy.dma_start(T.G[0:K, :], T.gath[0:K]).then_inc(S.gl, 16)
+        sc.wait_ge(S.arr2, K)
+        for k in range(K):
+            sc.dma_start(T.tp[:, 4 * k:4 * k + 4], T.gath[k]).then_inc(S.tpl, 16)
+        ve.wait_ge(S.tpl, 16 * K)
+    else:
+        sy.wait_ge(S.stc, 1)
+        sy.dma_start(T.coll[my_idx], T.st[:]).then_inc(S.own, 16)
+        g.wait_ge(S.arr1, arr1_total)
+        g.wait_ge(S.own, 16)
+        sent = _fold_call(g, core, T, topo, my_slot, n1, dests)
+        sc.wait_ge(S.arr1, arr1_total)
+        sc.wait_ge(S.own, 16)
+        sc.dma_start(T.G[0:n1, :], T.coll[0:n1]).then_inc(S.ge, 16)
+        te.wait_ge(S.ge, 16)
+        for j in range(4):
+            te.matmul(T.pta[:, j:j + 1], T.G[0:n1, j:512:4], T.ones[0:n1, 0:1], True, True).then_inc(S.pa, 1)
+        ve.wait_ge(S.pa, 4)
+        ve.tensor_copy(T.tp[:, 0:4], T.pta[:, 0:4]).then_inc(S.pac, 1)
+        other = 1 - my_slot
+        K = n1 + 1
+        sy.wait_ge(S.arr2, 1)
+        sy.dma_start(T.G[n1:K, :], T.gath[other]).then_inc(S.gl, 16)
+        sc.wait_ge(S.arr2, 1)
+        sc.dma_start(T.tp[:, 4:8], T.gath[other]).then_inc(S.tpl, 16)
+        ve.wait_ge(S.pac, 1)
+        ve.wait_ge(S.tpl, 16)
+
+    te.wait_ge(S.gl, 16)
+    pm = [T.pm0, T.pm1]
+    msem = [S.m0, S.m1]
+    for h in range(2):
+        for jj in range(2):
+            te.matmul(pm[h][:, jj:128:2], T.ones[0:K, 0:128], T.G[0:K, 256 * h + jj:256 * (h + 1):4],
+                      True, True).then_inc(msem[h], 1)
+    ve.tensor_tensor(T.tot[:], T.tp[:, 0:4], T.tp[:, 4:8], AluOpType.add).then_inc(S.tt, 1)
+    ve.wait_ge(S.tt, 1)
+    ve.tensor_tensor(T.msq[:, 0:2], T.tot[:, 0:2], T.tot[:, 0:2], AluOpType.mult).then_inc(S.tq, 1)
+    ve.wait_ge(S.m0, 2)
+    ve.tensor_tensor(T.ys[:, 0:128], T.xs[:, 0:128], T.pm0[:, 0:128], AluOpType.subtract).then_inc(S.y0, 1)
+    ve.wait_ge(S.tq, 1)
+    ve.tensor_tensor(T.sv[:, 0:2], T.tot[:, 2:4], T.msq[:, 0:2], AluOpType.subtract).then_inc(S.ts, 1)
+    ve.wait_ge(S.m1, 2)
+    ve.tensor_tensor(T.ys[:, 128:256], T.xs[:, 128:256], T.pm1[:, 0:128], AluOpType.subtract).then_inc(S.y1, 1)
+
+    sc.wait_ge(S.tt, 1)
+    sc.dma_start(T.m[:], T.tot[:, 0:2]).then_inc(S.outm, 16)
+    sy.wait_ge(S.y0, 1)
+    sy.dma_start(T.y[:, 0:128], T.ys[:, 0:128]).then_inc(S.outy0, 16)
+    sy.wait_ge(S.ts, 1)
+    sy.dma_start(T.s[:], T.sv[:, 0:2]).then_inc(S.outs, 16)
+    sc.wait_ge(S.y1, 1)
+    sc.dma_start(T.y[:, 128:256], T.ys[:, 128:256]).then_inc(S.outy1, 16)
+    g.wait_ge(S.sent, sent)
+    sy.wait_ge(S.outy0, 16)
+    sy.wait_ge(S.outs, 16)
+    sc.wait_ge(S.outm, 16)
+    sc.wait_ge(S.outy1, 16)

@@ -9,21 +9,30 @@ SCRATCH = {
     "ys": ("sbuf", [128, 256], "float32"),
     "invd": ("sbuf", [128, 4], "float32"),
     "ones": ("sbuf", [128, 128], "float32"),
-    "st": ("sbuf", [128, 4], "float32"),
-    "G": ("sbuf", [128, 512], "float32"),
-    "tp": ("sbuf", [128, 8], "float32"),
-    "tot": ("sbuf", [128, 4], "float32"),
-    "msq": ("sbuf", [128, 4], "float32"),
-    "sv": ("sbuf", [128, 4], "float32"),
-    "coll": ("dram", [16, 128, 4], "float32"),
-    "gath": ("dram", [2, 128, 4], "float32"),
-    "pst": ("psum", [128, 512], "float32"),
-    "pta": ("psum", [128, 512], "float32"),
+    "st0": ("sbuf", [128, 2], "float32"),
+    "st1": ("sbuf", [128, 2], "float32"),
+    "G0": ("sbuf", [128, 256], "float32"),
+    "G1": ("sbuf", [128, 256], "float32"),
+    "tp0": ("sbuf", [128, 32], "float32"),
+    "tp1": ("sbuf", [128, 32], "float32"),
+    "mt": ("sbuf", [128, 16], "float32"),
+    "msq": ("sbuf", [128, 16], "float32"),
+    "e2": ("sbuf", [128, 16], "float32"),
+    "sv": ("sbuf", [128, 16], "float32"),
+    "coll0": ("dram", [16, 128, 2], "float32"),
+    "coll1": ("dram", [16, 128, 2], "float32"),
+    "gath0": ("dram", [2, 128, 2], "float32"),
+    "gath1": ("dram", [2, 128, 2], "float32"),
+    "ps0": ("psum", [128, 512], "float32"),
+    "ps1": ("psum", [128, 512], "float32"),
+    "pta0": ("psum", [128, 512], "float32"),
+    "pta1": ("psum", [128, 512], "float32"),
     "pm0": ("psum", [128, 512], "float32"),
     "pm1": ("psum", [128, 512], "float32"),
 }
-SEMAPHORES = ["cst", "ld", "sq0", "sq1", "mm1", "stc", "sent", "arr1", "own", "ge", "pa", "pac", "arr2", "gl", "tpl",
-              "tt", "tq", "ts", "m0", "m1", "y0", "y1", "outm", "outs", "outy0", "outy1"]
+SEMAPHORES = ["cst", "ld", "sq0", "sq1", "mma", "mmb", "c0", "c1", "sent", "ar0", "ar1", "own0", "own1", "ge0", "ge1",
+              "pa0", "pa1", "pc0", "pc1", "fr0", "fr1", "gl", "tl0", "tl1", "tt", "tq", "te2", "ts", "m0", "m1",
+              "y0", "y1", "outm", "outs", "outy0", "outy1"]
 
 
 def _bits(mask):
@@ -47,18 +56,20 @@ def _plan(T, topo):
     for ch in sorted(by_chip):
         home = main if (ch == main or topo.same_plane(ch, main)) else ch
         groups.setdefault(home, []).extend(by_chip[ch])
-    relays = []
+    plans = [[], []]
     for home in sorted(groups):
         mem = groups[home]
         cand = [c for c in range(NSIM) if topo.chip(c) == home
                 and all(topo.may_write(c, r) for r in ranks if r != c)
                 and all(topo.may_write(m, c) for m in mem if m != c)]
         cand.sort(key=lambda c: (c in ranks, -sum(1 for m in mem if topo.die(m) == topo.die(c)), c))
-        relays.append((cand[0], mem))
-    return relays
+        for q in range(2):
+            plans[q].append((cand[q % len(cand)], mem))
+    return plans
 
 
-def _fold_call(g, core, T, topo, slot, nsrc, dests):
+def _fold_call(g, core, T, topo, q, slot, nsrc, dests):
+    coll, gath = T["coll%d" % q], T["gath%d" % q]
     load = {}
     order = sorted(dests, key=lambda d: (-_hops(topo, core, d), d))
     for d in order:
@@ -72,9 +83,9 @@ def _fold_call(g, core, T, topo, slot, nsrc, dests):
         for d in load[e]:
             rid, pid, _ = topo.addr(d)
             ids.append(DstId(rid=rid, pnc=pid))
-        transfers.append(RemoteDMATransfer(dst_ids=ids, dma_engine_mask=1 << e, remote_sem=T.sem.arr2,
-                                           srcs=[T.coll[i] for i in range(nsrc)],
-                                           dsts=[T.gath[slot] for _ in load[e]], alu_op=1))
+        transfers.append(RemoteDMATransfer(dst_ids=ids, dma_engine_mask=1 << e, remote_sem=T.sem["fr%d" % q],
+                                           srcs=[coll[i] for i in range(nsrc)],
+                                           dsts=[gath[slot] for _ in load[e]], alu_op=1))
     g.remote_dma_fused(transfers, local_sem=T.sem.sent)
     return len(transfers)
 
@@ -82,114 +93,144 @@ def _fold_call(g, core, T, topo, slot, nsrc, dests):
 def rank_program(g, core, T, topo):
     S = T.sem
     ranks = list(T.cores)
-    relays = _plan(T, topo)
+    plans = _plan(T, topo)
     rank = T.rank_of(core)
-    my_slot = None
-    for k, (rc, mem) in enumerate(relays):
-        if rc == core:
-            my_slot = k
-    if rank is None and my_slot is None:
+    role = [None, None]
+    for q in range(2):
+        for k, (rc, mem) in enumerate(plans[q]):
+            if rc == core:
+                role[q] = k
+    if rank is None and role == [None, None]:
         return
-    if my_slot is not None:
-        mem = relays[my_slot][1]
-        n1 = len(mem)
-        arr1_total = sum(len(_bits(topo.mask(m, core))) for m in mem if m != core)
-        dests = [r for r in ranks if r != core]
+    dests = [r for r in ranks if r != core]
+    n1 = [0, 0]
+    ar_total = [0, 0]
+    for q in range(2):
+        if role[q] is not None:
+            mem = plans[q][role[q]][1]
+            n1[q] = len(mem)
+            ar_total[q] = sum(len(_bits(topo.mask(m, core))) for m in mem if m != core)
 
+    sent = 0
     if rank is None:
-        g.wait_ge(S.arr1, arr1_total)
-        n = _fold_call(g, core, T, topo, my_slot, n1, dests)
-        g.wait_ge(S.sent, n)
+        for q in range(2):
+            if role[q] is not None:
+                g.wait_ge(S["ar%d" % q], ar_total[q])
+                sent += _fold_call(g, core, T, topo, q, role[q], n1[q], dests)
+        g.wait_ge(S.sent, sent)
         return
 
     sy, sc, te, ve = g.sync, g.scalar, g.tensor, g.vector
+    dq = [sy, sc]
     D = 128 * len(ranks)
-    for k, (rc, mem_k) in enumerate(relays):
-        if core in mem_k:
-            to_relay, my_idx = rc, mem_k.index(core)
+    is_relay = role != [None, None]
+    P, W = (128, 2) if is_relay else (16, 16)
 
     sy.dma_start(T.xs[:], T.x[:]).then_inc(S.ld, 16)
     ve.memset(T.invd[:], 1.0 / D).then_inc(S.cst, 1)
     ve.memset(T.ones[:], 1.0).then_inc(S.cst, 1)
-
     te.wait_ge(S.cst, 2)
     te.wait_ge(S.ld, 16)
     for jj in range(2):
-        te.matmul(T.pst[:, jj:jj + 1], T.xs[:, jj:256:2], T.invd[:, 0:1], True, True).then_inc(S.mm1, 1)
+        te.matmul(T.ps0[:, jj:jj + 1], T.xs[:, jj:256:2], T.invd[:, 0:1], True, True).then_inc(S.mma, 1)
     ve.wait_ge(S.ld, 16)
     ve.tensor_tensor(T.sq[:, 0:128], T.xs[:, 0:256:2], T.xs[:, 0:256:2], AluOpType.mult).then_inc(S.sq0, 1)
+    ve.wait_ge(S.mma, 2)
+    ve.tensor_copy(T.st0[:], T.ps0[:, 0:2]).then_inc(S.c0, 1)
     ve.tensor_tensor(T.sq[:, 128:256], T.xs[:, 1:256:2], T.xs[:, 1:256:2], AluOpType.mult).then_inc(S.sq1, 1)
     te.wait_ge(S.sq0, 1)
-    te.matmul(T.pst[:, 2:3], T.sq[:, 0:128], T.invd[:, 0:1], True, True).then_inc(S.mm1, 1)
+    te.matmul(T.ps1[:, 0:1], T.sq[:, 0:128], T.invd[:, 0:1], True, True).then_inc(S.mmb, 1)
     te.wait_ge(S.sq1, 1)
-    te.matmul(T.pst[:, 3:4], T.sq[:, 128:256], T.invd[:, 0:1], True, True).then_inc(S.mm1, 1)
-    ve.wait_ge(S.mm1, 4)
-    ve.tensor_copy(T.st[:], T.pst[:, 0:4]).then_inc(S.stc, 1)
+    te.matmul(T.ps1[:, 1:2], T.sq[:, 128:256], T.invd[:, 0:1], True, True).then_inc(S.mmb, 1)
+    ve.wait_ge(S.mmb, 2)
+    ve.tensor_copy(T.st1[:], T.ps1[:, 0:2]).then_inc(S.c1, 1)
 
-    if my_slot is None:
-        g.wait_ge(S.stc, 1)
-        rid, pid, _ = topo.addr(to_relay)
-        mask = topo.mask(core, to_relay)
-        g.remote_dma(out_ap=T.coll[my_idx], in_ap=T.st[:], remote_sem=S.arr1, local_sem=S.sent, pid=pid,
-                     routing_id=rid, dma_engine_mask=mask)
-        sent = len(_bits(mask))
-        K = len(relays)
-        sy.wait_ge(S.arr2, K)
-        sy.dma_start(T.G[0:K, :], T.gath[0:K]).then_inc(S.gl, 16)
-        sc.wait_ge(S.arr2, K)
-        for k in range(K):
-            sc.dma_start(T.tp[:, 4 * k:4 * k + 4], T.gath[k]).then_inc(S.tpl, 16)
-        ve.wait_ge(S.tpl, 16 * K)
-    else:
-        sy.wait_ge(S.stc, 1)
-        sy.dma_start(T.coll[my_idx], T.st[:]).then_inc(S.own, 16)
-        g.wait_ge(S.arr1, arr1_total)
-        g.wait_ge(S.own, 16)
-        sent = _fold_call(g, core, T, topo, my_slot, n1, dests)
-        sc.wait_ge(S.arr1, arr1_total)
-        sc.wait_ge(S.own, 16)
-        sc.dma_start(T.G[0:n1, :], T.coll[0:n1]).then_inc(S.ge, 16)
-        te.wait_ge(S.ge, 16)
-        for j in range(4):
-            te.matmul(T.pta[:, j:j + 1], T.G[0:n1, j:512:4], T.ones[0:n1, 0:1], True, True).then_inc(S.pa, 1)
-        ve.wait_ge(S.pa, 4)
-        ve.tensor_copy(T.tp[:, 0:4], T.pta[:, 0:4]).then_inc(S.pac, 1)
-        other = 1 - my_slot
-        K = n1 + 1
-        sy.wait_ge(S.arr2, 1)
-        sy.dma_start(T.G[n1:K, :], T.gath[other]).then_inc(S.gl, 16)
-        sc.wait_ge(S.arr2, 1)
-        sc.dma_start(T.tp[:, 4:8], T.gath[other]).then_inc(S.tpl, 16)
-        ve.wait_ge(S.pac, 1)
-        ve.wait_ge(S.tpl, 16)
+    for q in range(2):
+        for k, (rc, mem) in enumerate(plans[q]):
+            if core not in mem:
+                continue
+            idx = mem.index(core)
+            if rc == core:
+                dq[q].wait_ge(S["c%d" % q], 1)
+                dq[q].dma_start(T["coll%d" % q][idx], T["st%d" % q][:]).then_inc(S["own%d" % q], 16)
+            else:
+                g.wait_ge(S["c%d" % q], 1)
+                rid, pid, _ = topo.addr(rc)
+                mask = topo.mask(core, rc)
+                g.remote_dma(out_ap=T["coll%d" % q][idx], in_ap=T["st%d" % q][:], remote_sem=S["ar%d" % q],
+                             local_sem=S.sent, pid=pid, routing_id=rid, dma_engine_mask=mask)
+                sent += len(_bits(mask))
+    for q in range(2):
+        if role[q] is None:
+            continue
+        g.wait_ge(S["ar%d" % q], ar_total[q])
+        g.wait_ge(S["own%d" % q], 16)
+        sent += _fold_call(g, core, T, topo, q, role[q], n1[q], dests)
+        dq[q].wait_ge(S["ar%d" % q], ar_total[q])
+        dq[q].wait_ge(S["own%d" % q], 16)
+        dq[q].dma_start(T["G%d" % q][0:n1[q], :], T["coll%d" % q][0:n1[q]]).then_inc(S["ge%d" % q], 16)
 
-    te.wait_ge(S.gl, 16)
-    pm = [T.pm0, T.pm1]
-    msem = [S.m0, S.m1]
-    for h in range(2):
+    def presum(q):
+        te.wait_ge(S["ge%d" % q], 16)
         for jj in range(2):
-            te.matmul(pm[h][:, jj:128:2], T.ones[0:K, 0:128], T.G[0:K, 256 * h + jj:256 * (h + 1):4],
-                      True, True).then_inc(msem[h], 1)
-    ve.tensor_tensor(T.tot[:], T.tp[:, 0:4], T.tp[:, 4:8], AluOpType.add).then_inc(S.tt, 1)
-    ve.wait_ge(S.tt, 1)
-    ve.tensor_tensor(T.msq[:, 0:2], T.tot[:, 0:2], T.tot[:, 0:2], AluOpType.mult).then_inc(S.tq, 1)
-    ve.wait_ge(S.m0, 2)
-    ve.tensor_tensor(T.ys[:, 0:128], T.xs[:, 0:128], T.pm0[:, 0:128], AluOpType.subtract).then_inc(S.y0, 1)
-    ve.wait_ge(S.tq, 1)
-    ve.tensor_tensor(T.sv[:, 0:2], T.tot[:, 2:4], T.msq[:, 0:2], AluOpType.subtract).then_inc(S.ts, 1)
-    ve.wait_ge(S.m1, 2)
-    ve.tensor_tensor(T.ys[:, 128:256], T.xs[:, 128:256], T.pm1[:, 0:128], AluOpType.subtract).then_inc(S.y1, 1)
+            te.matmul(T["pta%d" % q][:, jj:jj + 1], T["G%d" % q][0:n1[q], jj:256:2], T.ones[0:n1[q], 0:1],
+                      True, True).then_inc(S["pa%d" % q], 1)
 
-    sc.wait_ge(S.tt, 1)
-    sc.dma_start(T.m[:], T.tot[:, 0:2]).then_inc(S.outm, 16)
+    nslot = len(plans[0])
+    nf = [nslot - (1 if role[q] is not None else 0) for q in range(2)]
+    sy.wait_ge(S.fr0, nf[0])
+    if role[0] is None:
+        K = nslot
+        sy.dma_start(T.G0[0:K, :], T.gath0[0:K]).then_inc(S.gl, 16)
+    else:
+        K = n1[0] + 1
+        sy.dma_start(T.G0[n1[0]:K, :], T.gath0[1 - role[0]]).then_inc(S.gl, 16)
+    for q in range(2):
+        sc.wait_ge(S["fr%d" % q], nf[q])
+        for k in range(nslot):
+            if k != role[q]:
+                sc.dma_start(T["tp%d" % q][0:P, 16 * k:16 * k + W], T["gath%d" % q][k]).then_inc(S["tl%d" % q], 16)
+
+    if role[0] is not None:
+        presum(0)
+    te.wait_ge(S.gl, 16)
+    te.matmul(T.pm0[:, 0:128], T.ones[0:K, 0:128], T.G0[0:K, 0:128], True, True).then_inc(S.m0, 1)
+    te.matmul(T.pm1[:, 0:128], T.ones[0:K, 0:128], T.G0[0:K, 128:256], True, True).then_inc(S.m1, 1)
+    if role[1] is not None:
+        presum(1)
+    ve.wait_ge(S.m0, 1)
+    ve.tensor_tensor(T.ys[:, 0:128], T.xs[:, 0:128], T.pm0[:, 0:128], AluOpType.subtract).then_inc(S.y0, 1)
+    ve.wait_ge(S.m1, 1)
+    ve.tensor_tensor(T.ys[:, 128:256], T.xs[:, 128:256], T.pm1[:, 0:128], AluOpType.subtract).then_inc(S.y1, 1)
     sy.wait_ge(S.y0, 1)
     sy.dma_start(T.y[:, 0:128], T.ys[:, 0:128]).then_inc(S.outy0, 16)
-    sy.wait_ge(S.ts, 1)
-    sy.dma_start(T.s[:], T.sv[:, 0:2]).then_inc(S.outs, 16)
-    sc.wait_ge(S.y1, 1)
-    sc.dma_start(T.y[:, 128:256], T.ys[:, 128:256]).then_inc(S.outy1, 16)
+    sy.wait_ge(S.y1, 1)
+    sy.dma_start(T.y[:, 128:256], T.ys[:, 128:256]).then_inc(S.outy1, 16)
+
+    for q in range(2):
+        if role[q] is not None:
+            k = role[q]
+            ve.wait_ge(S["pa%d" % q], 2)
+            ve.tensor_copy(T["tp%d" % q][:, 16 * k:16 * k + 2], T["pta%d" % q][:, 0:2]).then_inc(S["pc%d" % q], 1)
+    for q in range(2):
+        if role[q] is not None:
+            ve.wait_ge(S["pc%d" % q], 1)
+    ve.wait_ge(S.tl0, 16 * nf[0])
+    ve.tensor_tensor(T.mt[0:P, 0:W], T.tp0[0:P, 0:W], T.tp0[0:P, 16:16 + W], AluOpType.add).then_inc(S.tt, 1)
+    ve.wait_ge(S.tt, 1)
+    ve.tensor_tensor(T.msq[0:P, 0:W], T.mt[0:P, 0:W], T.mt[0:P, 0:W], AluOpType.mult).then_inc(S.tq, 1)
+    ve.wait_ge(S.tl1, 16 * nf[1])
+    ve.tensor_tensor(T.e2[0:P, 0:W], T.tp1[0:P, 0:W], T.tp1[0:P, 16:16 + W], AluOpType.add).then_inc(S.te2, 1)
+    ve.wait_ge(S.tq, 1)
+    ve.wait_ge(S.te2, 1)
+    ve.tensor_tensor(T.sv[0:P, 0:W], T.e2[0:P, 0:W], T.msq[0:P, 0:W], AluOpType.subtract).then_inc(S.ts, 1)
+    sy.wait_ge(S.tt, 1)
+    sy.dma_start(T.m[:], T.mt[0:P, 0:W]).then_inc(S.outm, 16)
+    sc.wait_ge(S.ts, 1)
+    sc.dma_start(T.s[:], T.sv[0:P, 0:W]).then_inc(S.outs, 16)
+
     g.wait_ge(S.sent, sent)
     sy.wait_ge(S.outy0, 16)
-    sy.wait_ge(S.outs, 16)
-    sc.wait_ge(S.outm, 16)
-    sc.wait_ge(S.outy1, 16)
+    sy.wait_ge(S.outy1, 16)
+    sy.wait_ge(S.outm, 16)
+    sc.wait_ge(S.outs, 16)

@@ -39,11 +39,15 @@ def _bits(mask):
     return [e for e in range(mask.bit_length()) if (mask >> e) & 1]
 
 
-def _hops(topo, a, b):
+def _route(topo, a, b):
     ca, cb = topo.chip(a), topo.chip(b)
     if ca == cb:
-        return 0
-    return 1 if (topo.mates(ca, cb) or topo.same_plane(ca, cb)) else 2
+        return (0, "chip")
+    if topo.mates(ca, cb):
+        return (1, "mate")
+    if topo.same_plane(ca, cb):
+        return (1, "plane")
+    return (2, "both")
 
 
 def _plan(T, topo):
@@ -64,30 +68,54 @@ def _plan(T, topo):
                 and all(topo.may_write(m, c) for m in mem if m != c)]
         cand.sort(key=lambda c: (c in ranks, -sum(1 for m in mem if topo.die(m) == topo.die(c)), c))
         for q in range(2):
-            plans[q].append((cand[q % len(cand)], mem))
+            c = cand[q % len(cand)]
+            plans[q].append((cand[0] if c in ranks else c, mem))
     return plans
+
+
+def _pow2(n):
+    p = 1
+    while 2 * p <= n:
+        p *= 2
+    return p
+
+
+def _groups(topo, core, dests):
+    routes = {}
+    for d in sorted(dests):
+        routes.setdefault(_route(topo, core, d), []).append(d)
+    off = sorted([r for r in routes if r[0] > 0], reverse=True)
+    out = []
+    used = 0
+    if off:
+        eng = _bits(topo.mask(core, routes[off[0]][0]))
+        share = _pow2(len(eng) // len(off))
+        for i, r in enumerate(off):
+            mask = sum(1 << e for e in eng[i * share:(i + 1) * share])
+            used |= mask
+            out.append((mask, routes[r]))
+    for r in routes:
+        if r[0] == 0:
+            eng = [e for e in _bits(topo.mask(core, routes[r][0])) if not (used >> e) & 1]
+            out.append((sum(1 << e for e in eng[-_pow2(len(eng)):]), routes[r]))
+    return out
 
 
 def _fold_call(g, core, T, topo, q, slot, nsrc, dests):
     coll, gath = T["coll%d" % q], T["gath%d" % q]
-    load = {}
-    order = sorted(dests, key=lambda d: (-_hops(topo, core, d), d))
-    for d in order:
-        allowed = _bits(topo.mask(core, d))
-        onchip = _hops(topo, core, d) == 0
-        e = min(allowed, key=lambda k: (len(load.get(k, [])), -k if onchip else k))
-        load.setdefault(e, []).append(d)
     transfers = []
-    for e in sorted(load):
+    n = 0
+    for mask, ds in _groups(topo, core, dests):
         ids = []
-        for d in load[e]:
+        for d in ds:
             rid, pid, _ = topo.addr(d)
             ids.append(DstId(rid=rid, pnc=pid))
-        transfers.append(RemoteDMATransfer(dst_ids=ids, dma_engine_mask=1 << e, remote_sem=T.sem["fr%d" % q],
+        transfers.append(RemoteDMATransfer(dst_ids=ids, dma_engine_mask=mask, remote_sem=T.sem["fr%d" % q],
                                            srcs=[coll[i] for i in range(nsrc)],
-                                           dsts=[gath[slot] for _ in load[e]], alu_op=1))
+                                           dsts=[gath[slot] for _ in ds], alu_op=1))
+        n += len(_bits(mask))
     g.remote_dma_fused(transfers, local_sem=T.sem.sent)
-    return len(transfers)
+    return n
 
 
 def rank_program(g, core, T, topo):
@@ -169,15 +197,26 @@ def rank_program(g, core, T, topo):
         dq[q].wait_ge(S["ar%d" % q], ar_total[q])
         dq[q].wait_ge(S["own%d" % q], 16)
         dq[q].dma_start(T["G%d" % q][0:n1[q], :], T["coll%d" % q][0:n1[q]]).then_inc(S["ge%d" % q], 16)
-
-    def presum(q):
         te.wait_ge(S["ge%d" % q], 16)
         for jj in range(2):
             te.matmul(T["pta%d" % q][:, jj:jj + 1], T["G%d" % q][0:n1[q], jj:256:2], T.ones[0:n1[q], 0:1],
                       True, True).then_inc(S["pa%d" % q], 1)
+        k = role[q]
+        ve.wait_ge(S["pa%d" % q], 2)
+        ve.tensor_copy(T["tp%d" % q][:, 16 * k:16 * k + 2], T["pta%d" % q][:, 0:2]).then_inc(S["pc%d" % q], 1)
+    for q in range(2):
+        if role[q] is not None:
+            ve.wait_ge(S["pc%d" % q], 1)
 
     nslot = len(plans[0])
-    nf = [nslot - (1 if role[q] is not None else 0) for q in range(2)]
+    nd = [nslot - (1 if role[q] is not None else 0) for q in range(2)]
+    nf = [0, 0]
+    for q in range(2):
+        for rc, mem in plans[q]:
+            if rc != core:
+                for mask, ds in _groups(topo, rc, [r for r in ranks if r != rc]):
+                    if core in ds:
+                        nf[q] += len(_bits(mask))
     sy.wait_ge(S.fr0, nf[0])
     if role[0] is None:
         K = nslot
@@ -191,46 +230,34 @@ def rank_program(g, core, T, topo):
             if k != role[q]:
                 sc.dma_start(T["tp%d" % q][0:P, 16 * k:16 * k + W], T["gath%d" % q][k]).then_inc(S["tl%d" % q], 16)
 
-    if role[0] is not None:
-        presum(0)
     te.wait_ge(S.gl, 16)
     te.matmul(T.pm0[:, 0:128], T.ones[0:K, 0:128], T.G0[0:K, 0:128], True, True).then_inc(S.m0, 1)
     te.matmul(T.pm1[:, 0:128], T.ones[0:K, 0:128], T.G0[0:K, 128:256], True, True).then_inc(S.m1, 1)
-    if role[1] is not None:
-        presum(1)
+    ve.wait_ge(S.tl0, 16 * nd[0])
+    ve.tensor_tensor(T.mt[0:P, 0:W], T.tp0[0:P, 0:W], T.tp0[0:P, 16:16 + W], AluOpType.add).then_inc(S.tt, 1)
+    ve.wait_ge(S.tt, 1)
+    ve.tensor_tensor(T.msq[0:P, 0:W], T.mt[0:P, 0:W], T.mt[0:P, 0:W], AluOpType.mult).then_inc(S.tq, 1)
     ve.wait_ge(S.m0, 1)
     ve.tensor_tensor(T.ys[:, 0:128], T.xs[:, 0:128], T.pm0[:, 0:128], AluOpType.subtract).then_inc(S.y0, 1)
     ve.wait_ge(S.m1, 1)
     ve.tensor_tensor(T.ys[:, 128:256], T.xs[:, 128:256], T.pm1[:, 0:128], AluOpType.subtract).then_inc(S.y1, 1)
-    sy.wait_ge(S.y0, 1)
-    sy.dma_start(T.y[:, 0:128], T.ys[:, 0:128]).then_inc(S.outy0, 16)
-    sy.wait_ge(S.y1, 1)
-    sy.dma_start(T.y[:, 128:256], T.ys[:, 128:256]).then_inc(S.outy1, 16)
-
-    for q in range(2):
-        if role[q] is not None:
-            k = role[q]
-            ve.wait_ge(S["pa%d" % q], 2)
-            ve.tensor_copy(T["tp%d" % q][:, 16 * k:16 * k + 2], T["pta%d" % q][:, 0:2]).then_inc(S["pc%d" % q], 1)
-    for q in range(2):
-        if role[q] is not None:
-            ve.wait_ge(S["pc%d" % q], 1)
-    ve.wait_ge(S.tl0, 16 * nf[0])
-    ve.tensor_tensor(T.mt[0:P, 0:W], T.tp0[0:P, 0:W], T.tp0[0:P, 16:16 + W], AluOpType.add).then_inc(S.tt, 1)
-    ve.wait_ge(S.tt, 1)
-    ve.tensor_tensor(T.msq[0:P, 0:W], T.mt[0:P, 0:W], T.mt[0:P, 0:W], AluOpType.mult).then_inc(S.tq, 1)
-    ve.wait_ge(S.tl1, 16 * nf[1])
+    ve.wait_ge(S.tl1, 16 * nd[1])
     ve.tensor_tensor(T.e2[0:P, 0:W], T.tp1[0:P, 0:W], T.tp1[0:P, 16:16 + W], AluOpType.add).then_inc(S.te2, 1)
     ve.wait_ge(S.tq, 1)
     ve.wait_ge(S.te2, 1)
     ve.tensor_tensor(T.sv[0:P, 0:W], T.e2[0:P, 0:W], T.msq[0:P, 0:W], AluOpType.subtract).then_inc(S.ts, 1)
+
     sy.wait_ge(S.tt, 1)
     sy.dma_start(T.m[:], T.mt[0:P, 0:W]).then_inc(S.outm, 16)
+    sy.wait_ge(S.y0, 1)
+    sy.dma_start(T.y[:, 0:128], T.ys[:, 0:128]).then_inc(S.outy0, 16)
+    sy.wait_ge(S.y1, 1)
+    sy.dma_start(T.y[:, 128:256], T.ys[:, 128:256]).then_inc(S.outy1, 16)
     sc.wait_ge(S.ts, 1)
     sc.dma_start(T.s[:], T.sv[0:P, 0:W]).then_inc(S.outs, 16)
 
     g.wait_ge(S.sent, sent)
+    sy.wait_ge(S.outm, 16)
     sy.wait_ge(S.outy0, 16)
     sy.wait_ge(S.outy1, 16)
-    sy.wait_ge(S.outm, 16)
     sc.wait_ge(S.outs, 16)

@@ -39,15 +39,11 @@ def _bits(mask):
     return [e for e in range(mask.bit_length()) if (mask >> e) & 1]
 
 
-def _route(topo, a, b):
+def _hops(topo, a, b):
     ca, cb = topo.chip(a), topo.chip(b)
     if ca == cb:
-        return (0, "chip")
-    if topo.mates(ca, cb):
-        return (1, "mate")
-    if topo.same_plane(ca, cb):
-        return (1, "plane")
-    return (2, "both")
+        return 0
+    return 1 if (topo.mates(ca, cb) or topo.same_plane(ca, cb)) else 2
 
 
 def _plan(T, topo):
@@ -81,23 +77,17 @@ def _pow2(n):
 
 
 def _groups(topo, core, dests):
-    routes = {}
-    for d in sorted(dests):
-        routes.setdefault(_route(topo, core, d), []).append(d)
-    off = sorted([r for r in routes if r[0] > 0], reverse=True)
+    order = sorted(dests, key=lambda d: (-_hops(topo, core, d), d))
+    off = [d for d in order if _hops(topo, core, d) > 0]
+    on = [d for d in order if _hops(topo, core, d) == 0]
     out = []
     used = 0
     if off:
-        eng = _bits(topo.mask(core, routes[off[0]][0]))
-        share = _pow2(len(eng) // len(off))
-        for i, r in enumerate(off):
-            mask = sum(1 << e for e in eng[i * share:(i + 1) * share])
-            used |= mask
-            out.append((mask, routes[r]))
-    for r in routes:
-        if r[0] == 0:
-            eng = [e for e in _bits(topo.mask(core, routes[r][0])) if not (used >> e) & 1]
-            out.append((sum(1 << e for e in eng[-_pow2(len(eng)):]), routes[r]))
+        used = topo.mask(core, off[0])
+        out.append((used, off))
+    if on:
+        eng = [e for e in _bits(topo.mask(core, on[0])) if not (used >> e) & 1]
+        out.append((sum(1 << e for e in eng[-_pow2(len(eng)):]), on))
     return out
 
 

from concourse.bass import DstId, RemoteDMATransfer
from concourse.mybir import AluOpType

NSIM = 64

SCRATCH = {
    "xs": ("sbuf", [128, 256], "float32"),
    "sq": ("sbuf", [128, 256], "float32"),
    "ys": ("sbuf", [128, 256], "float32"),
    "invd": ("sbuf", [128, 4], "float32"),
    "ones": ("sbuf", [128, 128], "float32"),
    "st0": ("sbuf", [128, 2], "float32"),
    "st1": ("sbuf", [128, 2], "float32"),
    "G0": ("sbuf", [128, 256], "float32"),
    "G1": ("sbuf", [128, 256], "float32"),
    "tp0": ("sbuf", [128, 32], "float32"),
    "tp1": ("sbuf", [128, 32], "float32"),
    "mt": ("sbuf", [128, 16], "float32"),
    "msq": ("sbuf", [128, 16], "float32"),
    "e2": ("sbuf", [128, 16], "float32"),
    "sv": ("sbuf", [128, 16], "float32"),
    "coll0": ("dram", [16, 128, 2], "float32"),
    "coll1": ("dram", [16, 128, 2], "float32"),
    "gath0": ("dram", [2, 128, 2], "float32"),
    "gath1": ("dram", [2, 128, 2], "float32"),
    "ps0": ("psum", [128, 512], "float32"),
    "ps1": ("psum", [128, 512], "float32"),
    "pta0": ("psum", [128, 512], "float32"),
    "pta1": ("psum", [128, 512], "float32"),
    "pm0": ("psum", [128, 512], "float32"),
    "pm1": ("psum", [128, 512], "float32"),
}
SEMAPHORES = ["cst", "ld", "sq0", "sq1", "mma", "mmb", "c0", "c1", "sent", "ar0", "ar1", "own0", "own1", "ge0", "ge1",
              "pa0", "pa1", "pc0", "pc1", "fr0", "fr1", "gl", "tl0", "tl1", "tt", "tq", "te2", "ts", "m0", "m1",
              "y0", "y1", "outm", "outs", "outy0", "outy1"]


def _bits(mask):
    return [e for e in range(mask.bit_length()) if (mask >> e) & 1]


def _hops(topo, a, b):
    ca, cb = topo.chip(a), topo.chip(b)
    if ca == cb:
        return 0
    return 1 if (topo.mates(ca, cb) or topo.same_plane(ca, cb)) else 2


def _plan(T, topo):
    ranks = list(T.cores)
    by_chip = {}
    for r in ranks:
        by_chip.setdefault(topo.chip(r), []).append(r)
    main = max(sorted(by_chip), key=lambda ch: len(by_chip[ch]))
    groups = {}
    for ch in sorted(by_chip):
        home = main if (ch == main or topo.same_plane(ch, main)) else ch
        groups.setdefault(home, []).extend(by_chip[ch])
    plans = [[], []]
    for home in sorted(groups):
        mem = groups[home]
        cand = [c for c in range(NSIM) if topo.chip(c) == home
                and all(topo.may_write(c, r) for r in ranks if r != c)
                and all(topo.may_write(m, c) for m in mem if m != c)]
        cand.sort(key=lambda c: (c in ranks, -sum(1 for m in mem if topo.die(m) == topo.die(c)), c))
        for q in range(2):
            c = cand[q % len(cand)]
            plans[q].append((cand[0] if c in ranks else c, mem))
    return plans


def _pow2(n):
    p = 1
    while 2 * p <= n:
        p *= 2
    return p


def _groups(topo, core, dests):
    order = sorted(dests, key=lambda d: (-_hops(topo, core, d), d))
    off = [d for d in order if _hops(topo, core, d) > 0]
    on = [d for d in order if _hops(topo, core, d) == 0]
    out = []
    used = 0
    if off:
        used = topo.mask(core, off[0])
        out.append((used, off))
    if on:
        eng = [e for e in _bits(topo.mask(core, on[0])) if not (used >> e) & 1]
        out.append((sum(1 << e for e in eng[-_pow2(len(eng)):]), on))
    return out


def _fold_call(g, core, T, topo, q, slot, nsrc, dests):
    coll, gath = T["coll%d" % q], T["gath%d" % q]
    transfers = []
    n = 0
    for mask, ds in _groups(topo, core, dests):
        ids = []
        for d in ds:
            rid, pid, _ = topo.addr(d)
            ids.append(DstId(rid=rid, pnc=pid))
        transfers.append(RemoteDMATransfer(dst_ids=ids, dma_engine_mask=mask, remote_sem=T.sem["fr%d" % q],
                                           srcs=[coll[i] for i in range(nsrc)],
                                           dsts=[gath[slot] for _ in ds], alu_op=1))
        n += len(_bits(mask))
    g.remote_dma_fused(transfers, local_sem=T.sem.sent)
    return n


def rank_program(g, core, T, topo):
    S = T.sem
    ranks = list(T.cores)
    plans = _plan(T, topo)
    rank = T.rank_of(core)
    role = [None, None]
    for q in range(2):
        for k, (rc, mem) in enumerate(plans[q]):
            if rc == core:
                role[q] = k
    if rank is None and role == [None, None]:
        return
    dests = [r for r in ranks if r != core]
    n1 = [0, 0]
    ar_total = [0, 0]
    for q in range(2):
        if role[q] is not None:
            mem = plans[q][role[q]][1]
            n1[q] = len(mem)
            ar_total[q] = sum(len(_bits(topo.mask(m, core))) for m in mem if m != core)

    sent = 0
    if rank is None:
        for q in range(2):
            if role[q] is not None:
                g.wait_ge(S["ar%d" % q], ar_total[q])
                sent += _fold_call(g, core, T, topo, q, role[q], n1[q], dests)
        g.wait_ge(S.sent, sent)
        return

    sy, sc, te, ve = g.sync, g.scalar, g.tensor, g.vector
    dq = [sy, sc]
    D = 128 * len(ranks)
    is_relay = role != [None, None]
    P, W = (128, 2) if is_relay else (16, 16)

    sy.dma_start(T.xs[:], T.x[:]).then_inc(S.ld, 16)
    ve.memset(T.invd[:], 1.0 / D).then_inc(S.cst, 1)
    ve.memset(T.ones[:], 1.0).then_inc(S.cst, 1)
    te.wait_ge(S.cst, 2)
    te.wait_ge(S.ld, 16)
    for jj in range(2):
        te.matmul(T.ps0[:, jj:jj + 1], T.xs[:, jj:256:2], T.invd[:, 0:1], True, True).then_inc(S.mma, 1)
    ve.wait_ge(S.ld, 16)
    ve.tensor_tensor(T.sq[:, 0:128], T.xs[:, 0:256:2], T.xs[:, 0:256:2], AluOpType.mult).then_inc(S.sq0, 1)
    ve.wait_ge(S.mma, 2)
    ve.tensor_copy(T.st0[:], T.ps0[:, 0:2]).then_inc(S.c0, 1)
    ve.tensor_tensor(T.sq[:, 128:256], T.xs[:, 1:256:2], T.xs[:, 1:256:2], AluOpType.mult).then_inc(S.sq1, 1)
    te.wait_ge(S.sq0, 1)
    te.matmul(T.ps1[:, 0:1], T.sq[:, 0:128], T.invd[:, 0:1], True, True).then_inc(S.mmb, 1)
    te.wait_ge(S.sq1, 1)
    te.matmul(T.ps1[:, 1:2], T.sq[:, 128:256], T.invd[:, 0:1], True, True).then_inc(S.mmb, 1)
    ve.wait_ge(S.mmb, 2)
    ve.tensor_copy(T.st1[:], T.ps1[:, 0:2]).then_inc(S.c1, 1)

    for q in range(2):
        for k, (rc, mem) in enumerate(plans[q]):
            if core not in mem:
                continue
            idx = mem.index(core)
            if rc == core:
                dq[q].wait_ge(S["c%d" % q], 1)
                dq[q].dma_start(T["coll%d" % q][idx], T["st%d" % q][:]).then_inc(S["own%d" % q], 16)
            else:
                g.wait_ge(S["c%d" % q], 1)
                rid, pid, _ = topo.addr(rc)
                mask = topo.mask(core, rc)
                g.remote_dma(out_ap=T["coll%d" % q][idx], in_ap=T["st%d" % q][:], remote_sem=S["ar%d" % q],
                             local_sem=S.sent, pid=pid, routing_id=rid, dma_engine_mask=mask)
                sent += len(_bits(mask))
    for q in range(2):
        if role[q] is None:
            continue
        g.wait_ge(S["ar%d" % q], ar_total[q])
        g.wait_ge(S["own%d" % q], 16)
        sent += _fold_call(g, core, T, topo, q, role[q], n1[q], dests)
        dq[q].wait_ge(S["ar%d" % q], ar_total[q])
        dq[q].wait_ge(S["own%d" % q], 16)
        dq[q].dma_start(T["G%d" % q][0:n1[q], :], T["coll%d" % q][0:n1[q]]).then_inc(S["ge%d" % q], 16)
        te.wait_ge(S["ge%d" % q], 16)
        for jj in range(2):
            te.matmul(T["pta%d" % q][:, jj:jj + 1], T["G%d" % q][0:n1[q], jj:256:2], T.ones[0:n1[q], 0:1],
                      True, True).then_inc(S["pa%d" % q], 1)
        k = role[q]
        ve.wait_ge(S["pa%d" % q], 2)
        ve.tensor_copy(T["tp%d" % q][:, 16 * k:16 * k + 2], T["pta%d" % q][:, 0:2]).then_inc(S["pc%d" % q], 1)
    for q in range(2):
        if role[q] is not None:
            ve.wait_ge(S["pc%d" % q], 1)

    nslot = len(plans[0])
    nd = [nslot - (1 if role[q] is not None else 0) for q in range(2)]
    nf = [0, 0]
    for q in range(2):
        for rc, mem in plans[q]:
            if rc != core:
                for mask, ds in _groups(topo, rc, [r for r in ranks if r != rc]):
                    if core in ds:
                        nf[q] += len(_bits(mask))
    sy.wait_ge(S.fr0, nf[0])
    if role[0] is None:
        K = nslot
        sy.dma_start(T.G0[0:K, :], T.gath0[0:K]).then_inc(S.gl, 16)
    else:
        K = n1[0] + 1
        sy.dma_start(T.G0[n1[0]:K, :], T.gath0[1 - role[0]]).then_inc(S.gl, 16)
    for q in range(2):
        sc.wait_ge(S["fr%d" % q], nf[q])
        for k in range(nslot):
            if k != role[q]:
                sc.dma_start(T["tp%d" % q][0:P, 16 * k:16 * k + W], T["gath%d" % q][k]).then_inc(S["tl%d" % q], 16)

    te.wait_ge(S.gl, 16)
    te.matmul(T.pm0[:, 0:128], T.ones[0:K, 0:128], T.G0[0:K, 0:128], True, True).then_inc(S.m0, 1)
    te.matmul(T.pm1[:, 0:128], T.ones[0:K, 0:128], T.G0[0:K, 128:256], True, True).then_inc(S.m1, 1)
    ve.wait_ge(S.tl0, 16 * nd[0])
    ve.tensor_tensor(T.mt[0:P, 0:W], T.tp0[0:P, 0:W], T.tp0[0:P, 16:16 + W], AluOpType.add).then_inc(S.tt, 1)
    ve.wait_ge(S.tt, 1)
    ve.tensor_tensor(T.msq[0:P, 0:W], T.mt[0:P, 0:W], T.mt[0:P, 0:W], AluOpType.mult).then_inc(S.tq, 1)
    ve.wait_ge(S.m0, 1)
    ve.tensor_tensor(T.ys[:, 0:128], T.xs[:, 0:128], T.pm0[:, 0:128], AluOpType.subtract).then_inc(S.y0, 1)
    ve.wait_ge(S.m1, 1)
    ve.tensor_tensor(T.ys[:, 128:256], T.xs[:, 128:256], T.pm1[:, 0:128], AluOpType.subtract).then_inc(S.y1, 1)
    ve.wait_ge(S.tl1, 16 * nd[1])
    ve.tensor_tensor(T.e2[0:P, 0:W], T.tp1[0:P, 0:W], T.tp1[0:P, 16:16 + W], AluOpType.add).then_inc(S.te2, 1)
    ve.wait_ge(S.tq, 1)
    ve.wait_ge(S.te2, 1)
    ve.tensor_tensor(T.sv[0:P, 0:W], T.e2[0:P, 0:W], T.msq[0:P, 0:W], AluOpType.subtract).then_inc(S.ts, 1)

    sy.wait_ge(S.tt, 1)
    sy.dma_start(T.m[:], T.mt[0:P, 0:W]).then_inc(S.outm, 16)
    sy.wait_ge(S.y0, 1)
    sy.dma_start(T.y[:, 0:128], T.ys[:, 0:128]).then_inc(S.outy0, 16)
    sy.wait_ge(S.y1, 1)
    sy.dma_start(T.y[:, 128:256], T.ys[:, 128:256]).then_inc(S.outy1, 16)
    sc.wait_ge(S.ts, 1)
    sc.dma_start(T.s[:], T.sv[0:P, 0:W]).then_inc(S.outs, 16)

    g.wait_ge(S.sent, sent)
    sy.wait_ge(S.outm, 16)
    sy.wait_ge(S.outy0, 16)
    sy.wait_ge(S.outy1, 16)
    sc.wait_ge(S.outs, 16)
